import numpy as np
import ml_dtypes


def mxq(x, axis, fmt="e4m3"):
    dtype, down = {"e4m3": (ml_dtypes.float8_e4m3fn, 7), "e5m2": (ml_dtypes.float8_e5m2, 14)}[fmt]
    v = np.moveaxis(np.asarray(x, np.float32).astype(ml_dtypes.bfloat16).astype(np.float64), axis, -1)
    blocks = v.reshape(v.shape[:-1] + (-1, 32))
    amax = np.abs(blocks).max(-1, keepdims=True)
    byte = np.maximum(np.where(amax > 0, np.frexp(amax)[1] - 1 + 127, 0) - down, 1)
    scale = np.exp2(byte - 127.0)
    codes = (blocks / scale).astype(np.float32).astype(dtype).astype(np.float64)
    return np.moveaxis((codes * scale).reshape(v.shape), -1, axis)


WIDE = False


def mx_kscale(k):
    if not WIDE:
        return np.ones(k)
    levels = np.array([10, -10, 5, -5, 0])
    if k % 512:
        return np.exp2(np.random.permutation(np.resize(levels, k // 32))).repeat(32)
    a = np.empty((k // 512, 16))
    for p in range(k // 512):
        a[p, :8] = np.random.permutation(np.resize(levels, 8))
        for g in range(8):
            far = levels[np.abs(levels - a[p, g]) >= 10]
            a[p, g + 8] = far[np.random.randint(len(far))]
    return np.exp2(a.ravel()).repeat(32)


def f64(x):
    return np.asarray(x).astype(np.float64)


def striped(idx):
    return np.tile(idx.reshape(-1, 16).T, (8, 1)).astype(np.uint16)


def unstriped(offs):
    return offs[:16].T.reshape(-1).astype(np.int64)


E2M1 = np.array([0.0, 0.5, 1.0, 1.5, 2.0, 3.0, 4.0, 6.0, -0.0, -0.5, -1.0, -1.5, -2.0, -3.0, -4.0, -6.0])


def pack_weight(w, fmt):
    k, n = w.shape
    w = f64(np.asarray(w, np.float32).astype(ml_dtypes.bfloat16)).reshape(k // 32, 32, n)
    amax = np.abs(w).max(1)
    if fmt == "e4m3":
        byte = np.frexp(amax)[1] - 1 + 127 - 7
    else:
        mant, ex = np.frexp(amax / 6.0)
        byte = np.where(mant > 0.5, ex, ex - 1) + 127
    byte = np.clip(np.where(amax > 0, byte, 1), 1, 254)
    scaled = (w * np.exp2(127.0 - byte)[:, None, :]).reshape(k, n).astype(np.float32)
    by_word = np.ascontiguousarray(scaled.reshape(k // 512, 128, 4, n).transpose(0, 1, 3, 2))
    if fmt == "e4m3":
        words = by_word.astype(ml_dtypes.float8_e4m3fn).view(np.uint8)
    else:
        c = by_word.astype(ml_dtypes.float4_e2m1fn).view(np.uint8) & 0xF
        words = (c[..., 0::2] | (c[..., 1::2] << 4)).reshape(k // 512, 128, 2 * n)
    return np.ascontiguousarray(words), np.ascontiguousarray(byte.astype(np.uint8).reshape(k // 512, 16, n))


def unpack_weight(words, scales, fmt):
    g, _, n = scales.shape
    words = np.ascontiguousarray(words).reshape(g, 128, n, -1)
    if fmt == "e4m3":
        vals = words.view(ml_dtypes.float8_e4m3fn).astype(np.float64)
    else:
        nib = np.empty((g, 128, n, 4), np.uint8)
        nib[..., 0::2] = words & 0xF
        nib[..., 1::2] = words >> 4
        vals = E2M1[nib]
    vals = vals * np.repeat(np.exp2(scales.astype(np.float64) - 127.0), 8, axis=1)[..., None]
    return vals.transpose(0, 1, 3, 2).reshape(g * 512, n)


def relu(v):
    return np.maximum(v, 0.0)


K, T, E, C, N = 1024, 1536, 12, 256, 256


def by_expert(wq, xq):
    return np.concatenate([wq[e].T @ xq[:, e * C:(e + 1) * C] for e in range(E)], axis=1)


def setup_inputs():
    n = np.random.standard_normal
    s = mx_kscale(K)[:, None]
    first = np.random.permutation(np.repeat(np.arange(E), T // E))
    second = (first + 1 + np.random.permutation(np.repeat(np.arange(E - 1), -(-T // (E - 1)))[:T])) % E
    while np.bincount(second, minlength=E).max() != T // E:
        load = np.bincount(second, minlength=E); hi, lo = int(load.argmax()), int(load.argmin())
        t = np.flatnonzero((second == hi) & (first != lo))[0]; second[t] = lo
    slot_token = np.empty(E * C, np.int64); pos = np.empty((2, T), np.int64); fill = np.zeros(E, np.int64)
    place = np.stack([np.random.permutation(C) for _ in range(E)])
    for r, deal in enumerate((first, second)):
        for t in np.random.permutation(T):
            e = deal[t]; j = e * C + place[e, fill[e]]; fill[e] += 1; slot_token[j] = t; pos[r, t] = j
    g = np.random.uniform(0.2, 0.8, T)
    x = pack_weight(n((K, T)) * s, "e4m3")
    return {
        "x_words": x[0],
        "x_scales": x[1],
        "w": (n((E, K, N)) / np.sqrt(K) / s[None]).astype(np.float32),
        "b": (0.3 * n((N, E))).astype(np.float32),
        "gate": np.stack([np.tile(g, (N, 1)), np.tile(1.0 - g, (N, 1))]).astype(np.float32),
        "offs": striped(slot_token),
        "pos1": striped(pos[0]),
        "pos2": striped(pos[1]),
    }


def reference(x_words, x_scales, w, b, gate, offs, pos1, pos2):
    idx = unstriped(offs)
    xq = unpack_weight(x_words, x_scales, "e4m3")[:, idx]
    y = by_expert(mxq(f64(w), 1, "e4m3"), xq)
    y = relu(y + np.repeat(f64(b), C, axis=1))
    return f64(gate[0]) * y[:, unstriped(pos1)] + f64(gate[1]) * y[:, unstriped(pos2)]

@@ -1,0 +1,189 @@
+from contextlib import ExitStack
+
+import concourse.mybir as mybir
+from concourse.masks import make_identity
+
+K, T, E, C, N = 1024, 1536, 12, 256, 256
+SLOTS = E * C
+FLOPS = 2 * K * N * SLOTS
+BYTES = K * T + K * T // 32 + 4 * E * K * N + 4 * N * E + 4 * 2 * T + 2 * 128 * (SLOTS + 2 * T) // 16 + 4 * N * T
+
+F32 = mybir.dt.float32
+BF16 = mybir.dt.bfloat16
+I32 = mybir.dt.int32
+U32 = mybir.dt.uint32
+U16 = mybir.dt.uint16
+U8 = mybir.dt.uint8
+FP8X4 = mybir.dt.float8_e4m3fn_x4
+ACT = mybir.ActivationFunctionType
+ALU = mybir.AluOpType
+
+P = 128
+PACK = 4
+PASSES = K // (P * PACK)
+HALVES = N // P
+PER_COL = 16
+GATE_COLS = T // P
+LEAD = 3
+EARLY_EVERY = 4
+RELU_LAG_FIRST = 3
+RELU_LAG_SECOND = 2
+VECTOR_CASTS = 1
+CHUNKS_FIRST = (512, 512, 512)
+CHUNKS_SECOND = (512, 512, 256, 256)
+
+
+def unit_order():
+    units, early = [], 0
+    for e in range(E):
+        units.append((e, 0))
+        if e % EARLY_EVERY == EARLY_EVERY - 1 and e < E - 1:
+            units.append((early, 1))
+            early = early + 1
+    return units + [(e, 1) for e in range(early, E)]
+
+
+def tile_moe_pkd_lin_relu_kernel(tc, x_words, x_scales, w, b, gate, offs, pos1, pos2, out):
+    nc = tc.nc
+    units = unit_order()
+    last_first = units.index((E - 1, 0))
+
+    with ExitStack() as ctx:
+        lists = ctx.enter_context(tc.tile_pool(name="lists", bufs=1))
+        keep = ctx.enter_context(tc.tile_pool(name="keep", bufs=1))
+        ring = ctx.enter_context(tc.tile_pool(name="ring", bufs=6))
+        gate_psum = ctx.enter_context(tc.psum_pool(name="gate_psum", bufs=2))
+        sum_psum = ctx.enter_context(tc.psum_pool(name="sum_psum", bufs=6))
+
+        offs_sb = lists.tile([P, SLOTS // PER_COL], U16, name="offs_sb")
+        nc.sync.dma_start(offs_sb[:], offs)
+
+        xs_sb = keep.tile([P, T], U8, name="xs_sb", align_bytes=64)
+        nc.vector.memset(xs_sb[:].bitcast(I32), 0)
+        for quad in range(4):
+            nc.sync.dma_start(
+                out=xs_sb[32 * quad : 32 * quad + 4 * PASSES, :].bitcast(I32),
+                in_=x_scales[:, 4 * quad : 4 * quad + 4, :].bitcast(I32),
+            )
+
+        gate_col = keep.tile([P, 2, GATE_COLS], F32, name="gate_col")
+        nc.sync.dma_start(out=gate_col[:], in_=gate[:, 0, :].rearrange("r (p c) -> p r c", p=P))
+
+        xw_sb = []
+        for o in range(PASSES):
+            xw = keep.tile([P, T], I32, name=f"xw{o}", align_bytes=64)
+            nc.sync.dma_start(out=xw[:], in_=x_words[o].rearrange("p t r -> p (t r)").bitcast(I32))
+            xw_sb.append(xw)
+
+        raw = []
+        bias = keep.tile([P, HALVES, E], F32, name="bias")
+        pos_sb = [lists.tile([P, T // PER_COL], U16, name=f"pos{r}_sb") for r in range(2)]
+        for i, (e, h) in enumerate(units):
+            tile = keep.tile([P, PASSES, PACK, P], F32, name=f"raw{i}")
+            rows = w[e].rearrange("(o p j) n -> o p j n", o=PASSES, j=PACK)
+            for o in range(PASSES):
+                nc.sync.dma_start(out=tile[:, o], in_=rows[o, :, :, h * P : (h + 1) * P])
+            raw.append(tile)
+            if i == 0:
+                nc.sync.dma_start(out=bias[:], in_=b.rearrange("(h p) e -> p h e", p=P))
+            if i == LEAD:
+                nc.sync.dma_start(pos_sb[0][:], pos1)
+                nc.sync.dma_start(pos_sb[1][:], pos2)
+
+        ident = keep.tile([P, P], F32, name="ident")
+        make_identity(nc, ident[:])
+        gate_sb = [keep.tile([P, T], F32, name=f"gate{r}") for r in range(2)]
+        for r in range(2):
+            for c0 in range(0, GATE_COLS, 4):
+                spread = gate_psum.tile([P, 4, P], F32, name="spread")
+                for j in range(4):
+                    nc.tensor.transpose(spread[:, j, :], gate_col[:, r, c0 + j : c0 + j + 1].to_broadcast([P, P]), ident[:])
+                nc.scalar.copy(
+                    out=gate_sb[r][:].rearrange("m (k c) -> m k c", c=GATE_COLS)[:, :, c0 : c0 + 4],
+                    in_=spread[:].rearrange("m j k -> m k j"),
+                )
+
+        y_sb = [keep.tile([P, SLOTS], F32, name=f"y{h}") for h in range(HALVES)]
+        tok_words, tok_scales, sums = {}, {}, {}
+
+        def gather_tokens(e, words_tag, scales_tag):
+            slots = offs_sb[:, e * C // PER_COL : (e + 1) * C // PER_COL]
+            scales = keep.tile([P, C], U8, name=f"tok_scales{e}", tag=scales_tag, align_bytes=64)
+            nc.vector.tensor_copy(scales[:], xs_sb[:].indirect(slots))
+            words = keep.tile([P, PASSES * C], U32, name=f"tok_words{e}", tag=words_tag, align_bytes=64)
+            for o in range(PASSES):
+                nc.vector.tensor_copy(words[:, o * C : (o + 1) * C], xw_sb[o][:].bitcast(U32).indirect(slots))
+            tok_words[e], tok_scales[e] = words, scales
+
+        def multiply(i):
+            e, h = units[i]
+            grouped = keep.tile([P, PASSES, P, PACK], BF16, name=f"grouped{i}", tag=f"wide{i}", align_bytes=64)
+            dst = grouped[:].rearrange("p o (c i) j -> p o c j i", i=4)
+            src = raw[i][:].rearrange("p o j (c i) -> p o c j i", i=4)
+            if i >= len(units) - VECTOR_CASTS:
+                nc.vector.tensor_copy(out=dst, in_=src)
+            else:
+                nc.scalar.copy(out=dst, in_=src)
+            codes = ring.tile([P, PASSES * P], U32, name="codes", align_bytes=64)
+            w_scales = keep.tile([P, PASSES * P], U8, name=f"w_scales{i}", tag=f"narrow{i}", align_bytes=64)
+            nc.vector.quantize_mx(
+                out=codes[:].bitcast(FP8X4), scales=w_scales[:], in_=grouped[:].rearrange("p o n j -> p (o n j)")
+            )
+            acc = sum_psum.tile([P, C], F32, name="acc")
+            for o in range(PASSES):
+                nc.tensor.matmul_mx(
+                    out=acc[:],
+                    lhsT=codes[:, o * P : (o + 1) * P].bitcast(FP8X4),
+                    lhsT_scale=w_scales[:, o * P : (o + 1) * P],
+                    rhs=tok_words[e][:, o * C : (o + 1) * C].bitcast(FP8X4),
+                    rhs_scale=tok_scales[e][4 * o : P, :],
+                    start=(o == 0),
+                    stop=(o == PASSES - 1),
+                )
+            sums[i] = acc
+
+        def finish(i):
+            e, h = units[i]
+            nc.scalar.activation(
+                out=y_sb[h][:, e * C : (e + 1) * C], in_=sums[i][:], func=ACT.Relu, bias=bias[:, h, e : e + 1], scale=1.0
+            )
+
+        def weighted(h, r, t0, width, tag):
+            part = keep.tile([P, width], F32, name=f"part{h}_{r}_{t0}", tag=tag, align_bytes=64)
+            picks = pos_sb[r][:, t0 // PER_COL : (t0 + width) // PER_COL]
+            nc.vector.tensor_tensor(part[:], y_sb[h][:].indirect(picks), gate_sb[r][:, t0 : t0 + width], ALU.mult)
+            return part
+
+        def add_and_store(h, t0, width, first, second):
+            nc.vector.tensor_tensor(first[:], first[:], second[:], ALU.add)
+            nc.sync.dma_start(out=out[h * P : (h + 1) * P, t0 : t0 + width], in_=first[:])
+
+        for e in range(LEAD):
+            gather_tokens(e, f"first_words{e}", f"first_scales{e}")
+
+        last_scalar = len(units) - 1 - VECTOR_CASTS
+        jobs = [(sum(CHUNKS_FIRST[:c]), width, r) for c, width in enumerate(CHUNKS_FIRST) for r in range(2)]
+        job_at = {
+            last_first + 1 + round(k * (last_scalar - last_first - 1) / (len(jobs) - 1)): job for k, job in enumerate(jobs)
+        }
+        relu_at = [
+            min(i + RELU_LAG_FIRST, last_first + 1) if i <= last_first else min(i + RELU_LAG_SECOND, len(units) - 1)
+            for i in range(len(units))
+        ]
+        held = {}
+        for i, (e, h) in enumerate(units):
+            multiply(i)
+            if h == 0 and e + LEAD < E:
+                gather_tokens(e + LEAD, f"wide{i}", f"narrow{i}")
+            for done in range(len(units)):
+                if relu_at[done] == i:
+                    finish(done)
+            if i in job_at:
+                t0, width, r = job_at[i]
+                held[r] = weighted(0, r, t0, width, f"wide{i}")
+                if r == 1:
+                    add_and_store(0, t0, width, held[0], held[1])
+
+        for c, width in enumerate(CHUNKS_SECOND):
+            t0 = sum(CHUNKS_SECOND[:c])
+            add_and_store(1, t0, width, *[weighted(1, r, t0, width, f"last{c}_{r}") for r in range(2)])

@@ -24,34 +24,31 @@ PASSES = K // (P * PACK)
 HALVES = N // P
 PER_COL = 16
 GATE_COLS = T // P
-LEAD = 3
-EARLY_EVERY = 4
+GROUP = 2
+LEAD = 2
+SPLIT = 3
+EARLY = 5
+RELU_LAG_WIDE = 2
 RELU_LAG_FIRST = 3
 RELU_LAG_SECOND = 2
-VECTOR_CASTS = 1
 CHUNKS_FIRST = (512, 512, 512)
 CHUNKS_SECOND = (512, 512, 256, 256)
 
 
 def unit_order():
-    units, early = [], 0
-    for e in range(E):
-        units.append((e, 0))
-        if e % EARLY_EVERY == EARLY_EVERY - 1 and e < E - 1:
-            units.append((early, 1))
-            early = early + 1
-    return units + [(e, 1) for e in range(early, E)]
+    first = [(e, 0, HALVES if e < EARLY else 1) for e in range(E)]
+    return first + [(e, 1, 1) for e in range(EARLY, E)]
 
 
 def tile_moe_pkd_lin_relu_kernel(tc, x_words, x_scales, w, b, gate, offs, pos1, pos2, out):
     nc = tc.nc
     units = unit_order()
-    last_first = units.index((E - 1, 0))
+    last_first = E - 1
 
     with ExitStack() as ctx:
         lists = ctx.enter_context(tc.tile_pool(name="lists", bufs=1))
         keep = ctx.enter_context(tc.tile_pool(name="keep", bufs=1))
-        ring = ctx.enter_context(tc.tile_pool(name="ring", bufs=6))
+        ring = ctx.enter_context(tc.tile_pool(name="ring", bufs=4))
         gate_psum = ctx.enter_context(tc.psum_pool(name="gate_psum", bufs=2))
         sum_psum = ctx.enter_context(tc.psum_pool(name="sum_psum", bufs=6))
 
@@ -69,26 +66,34 @@ def tile_moe_pkd_lin_relu_kernel(tc, x_words, x_scales, w, b, gate, offs, pos1, 
         gate_col = keep.tile([P, 2, GATE_COLS], F32, name="gate_col")
         nc.sync.dma_start(out=gate_col[:], in_=gate[:, 0, :].rearrange("r (p c) -> p r c", p=P))
 
-        xw_sb = []
-        for o in range(PASSES):
-            xw = keep.tile([P, T], I32, name=f"xw{o}", align_bytes=64)
-            nc.sync.dma_start(out=xw[:], in_=x_words[o].rearrange("p t r -> p (t r)").bitcast(I32))
-            xw_sb.append(xw)
+        xw_sb = [keep.tile([P, T], I32, name=f"xw{o}", align_bytes=64) for o in range(PASSES)]
 
-        raw = []
+        def load_words(o):
+            nc.sync.dma_start(out=xw_sb[o][:], in_=x_words[o].rearrange("p t r -> p (t r)").bitcast(I32))
+
+        load_words(0)
+        raw = {}
         bias = keep.tile([P, HALVES, E], F32, name="bias")
         pos_sb = [lists.tile([P, T // PER_COL], U16, name=f"pos{r}_sb") for r in range(2)]
-        for i, (e, h) in enumerate(units):
-            tile = keep.tile([P, PASSES, PACK, P], F32, name=f"raw{i}")
-            rows = w[e].rearrange("(o p j) n -> o p j n", o=PASSES, j=PACK)
+        rows = w.rearrange("e (o p j) n -> e o p j n", o=PASSES, j=PACK)
+        for e in range(E - SPLIT):
+            both = keep.tile([P, PASSES, PACK, N], F32, name=f"raw{e}")
             for o in range(PASSES):
-                nc.sync.dma_start(out=tile[:, o], in_=rows[o, :, :, h * P : (h + 1) * P])
-            raw.append(tile)
-            if i == 0:
+                nc.sync.dma_start(out=both[:, o], in_=rows[e, o])
+            for h in range(HALVES):
+                raw[e, h] = both[:, :, :, h * P :]
+            if e == 0:
+                load_words(1)
                 nc.sync.dma_start(out=bias[:], in_=b.rearrange("(h p) e -> p h e", p=P))
-            if i == LEAD:
+            if e == 3:
                 nc.sync.dma_start(pos_sb[0][:], pos1)
                 nc.sync.dma_start(pos_sb[1][:], pos2)
+        for h in range(HALVES):
+            for e in range(E - SPLIT, E):
+                half = keep.tile([P, PASSES, PACK, P], F32, name=f"raw{e}_{h}")
+                for o in range(PASSES):
+                    nc.sync.dma_start(out=half[:, o], in_=rows[e, o, :, :, h * P : (h + 1) * P])
+                raw[e, h] = half[:]
 
         ident = keep.tile([P, P], F32, name="ident")
         make_identity(nc, ident[:])
@@ -106,47 +111,60 @@ def tile_moe_pkd_lin_relu_kernel(tc, x_words, x_scales, w, b, gate, offs, pos1, 
         y_sb = [keep.tile([P, SLOTS], F32, name=f"y{h}") for h in range(HALVES)]
         tok_words, tok_scales, sums = {}, {}, {}
 
-        def gather_tokens(e, words_tag, scales_tag):
-            slots = offs_sb[:, e * C // PER_COL : (e + 1) * C // PER_COL]
-            scales = keep.tile([P, C], U8, name=f"tok_scales{e}", tag=scales_tag, align_bytes=64)
+        def gather_tokens(g, words_tag, scales_tag):
+            width = GROUP * C
+            slots = offs_sb[:, g * width // PER_COL : (g + 1) * width // PER_COL]
+            scales = keep.tile([P, width], U8, name=f"tok_scales{g}", tag=scales_tag, align_bytes=64)
             nc.vector.tensor_copy(scales[:], xs_sb[:].indirect(slots))
-            words = keep.tile([P, PASSES * C], U32, name=f"tok_words{e}", tag=words_tag, align_bytes=64)
+            words = keep.tile([P, PASSES * width], U32, name=f"tok_words{g}", tag=words_tag, align_bytes=64)
             for o in range(PASSES):
-                nc.vector.tensor_copy(words[:, o * C : (o + 1) * C], xw_sb[o][:].bitcast(U32).indirect(slots))
-            tok_words[e], tok_scales[e] = words, scales
+                nc.vector.tensor_copy(words[:, o * width : (o + 1) * width], xw_sb[o][:].bitcast(U32).indirect(slots))
+            for k in range(GROUP):
+                tok_scales[g * GROUP + k] = scales[:, k * C : (k + 1) * C]
+                tok_words[g * GROUP + k] = [words[:, o * width + k * C : o * width + (k + 1) * C] for o in range(PASSES)]
 
         def multiply(i):
-            e, h = units[i]
-            grouped = keep.tile([P, PASSES, P, PACK], BF16, name=f"grouped{i}", tag=f"wide{i}", align_bytes=64)
+            e, h0, count = units[i]
+            cols = count * P
+            grouped = keep.tile([P, PASSES, cols, PACK], BF16, name=f"grouped{i}", tag=f"wide{i}", align_bytes=64)
             dst = grouped[:].rearrange("p o (c i) j -> p o c j i", i=4)
-            src = raw[i][:].rearrange("p o j (c i) -> p o c j i", i=4)
-            if i >= len(units) - VECTOR_CASTS:
-                nc.vector.tensor_copy(out=dst, in_=src)
+            src = raw[e, h0][:, :, :, :cols].rearrange("p o j (c i) -> p o c j i", i=4)
+            if i == last_first:
+                for o in range(PASSES):
+                    nc.vector.tensor_copy(out=dst[:, o], in_=src[:, o])
             else:
                 nc.scalar.copy(out=dst, in_=src)
-            codes = ring.tile([P, PASSES * P], U32, name="codes", align_bytes=64)
-            w_scales = keep.tile([P, PASSES * P], U8, name=f"w_scales{i}", tag=f"narrow{i}", align_bytes=64)
+            codes = ring.tile([P, PASSES * cols], U32, name="codes", align_bytes=64)
+            w_scales = keep.tile([P, PASSES * cols], U8, name=f"w_scales{i}", tag=f"narrow{i}", align_bytes=64)
             nc.vector.quantize_mx(
                 out=codes[:].bitcast(FP8X4), scales=w_scales[:], in_=grouped[:].rearrange("p o n j -> p (o n j)")
             )
-            acc = sum_psum.tile([P, C], F32, name="acc")
-            for o in range(PASSES):
-                nc.tensor.matmul_mx(
-                    out=acc[:],
-                    lhsT=codes[:, o * P : (o + 1) * P].bitcast(FP8X4),
-                    lhsT_scale=w_scales[:, o * P : (o + 1) * P],
-                    rhs=tok_words[e][:, o * C : (o + 1) * C].bitcast(FP8X4),
-                    rhs_scale=tok_scales[e][4 * o : P, :],
-                    start=(o == 0),
-                    stop=(o == PASSES - 1),
-                )
+            acc = sum_psum.tile([P, count, C], F32, name="acc")
+            for k in range(count):
+                for o in range(PASSES):
+                    w_cols = slice(o * cols + k * P, o * cols + (k + 1) * P)
+                    nc.tensor.matmul_mx(
+                        out=acc[:, k, :],
+                        lhsT=codes[:, w_cols].bitcast(FP8X4),
+                        lhsT_scale=w_scales[:, w_cols],
+                        rhs=tok_words[e][o].bitcast(FP8X4),
+                        rhs_scale=tok_scales[e][4 * o : P, :],
+                        start=(o == 0),
+                        stop=(o == PASSES - 1),
+                    )
             sums[i] = acc
 
         def finish(i):
-            e, h = units[i]
-            nc.scalar.activation(
-                out=y_sb[h][:, e * C : (e + 1) * C], in_=sums[i][:], func=ACT.Relu, bias=bias[:, h, e : e + 1], scale=1.0
-            )
+            e, h0, count = units[i]
+            for k in range(count):
+                h = h0 + k
+                nc.scalar.activation(
+                    out=y_sb[h][:, e * C : (e + 1) * C],
+                    in_=sums[i][:, k, :],
+                    func=ACT.Relu,
+                    bias=bias[:, h, e : e + 1],
+                    scale=1.0,
+                )
 
         def weighted(h, r, t0, width, tag):
             part = keep.tile([P, width], F32, name=f"part{h}_{r}_{t0}", tag=tag, align_bytes=64)
@@ -158,31 +176,28 @@ def tile_moe_pkd_lin_relu_kernel(tc, x_words, x_scales, w, b, gate, offs, pos1, 
             nc.vector.tensor_tensor(first[:], first[:], second[:], ALU.add)
             nc.sync.dma_start(out=out[h * P : (h + 1) * P, t0 : t0 + width], in_=first[:])
 
-        for e in range(LEAD):
-            gather_tokens(e, f"first_words{e}", f"first_scales{e}")
+        for g in range(LEAD):
+            gather_tokens(g, f"first_words{g}", f"first_scales{g}")
 
-        last_scalar = len(units) - 1 - VECTOR_CASTS
         jobs = [(sum(CHUNKS_FIRST[:c]), width, r) for c, width in enumerate(CHUNKS_FIRST) for r in range(2)]
-        job_at = {
-            last_first + 1 + round(k * (last_scalar - last_first - 1) / (len(jobs) - 1)): job for k, job in enumerate(jobs)
-        }
+        job_at = [min(last_first + 1 + k, len(units) - 1) for k in range(len(jobs))]
         relu_at = [
-            min(i + RELU_LAG_FIRST, last_first + 1) if i <= last_first else min(i + RELU_LAG_SECOND, len(units) - 1)
+            min(i + (RELU_LAG_WIDE if i < EARLY else RELU_LAG_FIRST), last_first + 1) if i <= last_first else min(i + RELU_LAG_SECOND, len(units) - 1)
             for i in range(len(units))
         ]
         held = {}
-        for i, (e, h) in enumerate(units):
+        for i in range(len(units)):
             multiply(i)
-            if h == 0 and e + LEAD < E:
-                gather_tokens(e + LEAD, f"wide{i}", f"narrow{i}")
+            if i % GROUP == 0 and LEAD + i // GROUP < E // GROUP:
+                gather_tokens(LEAD + i // GROUP, f"wide{i}", f"narrow{i}")
             for done in range(len(units)):
                 if relu_at[done] == i:
                     finish(done)
-            if i in job_at:
-                t0, width, r = job_at[i]
-                held[r] = weighted(0, r, t0, width, f"wide{i}")
-                if r == 1:
-                    add_and_store(0, t0, width, held[0], held[1])
+            for k, (t0, width, r) in enumerate(jobs):
+                if job_at[k] == i:
+                    held[r] = weighted(0, r, t0, width, f"wide{i}" if last_first + 1 + k == i else f"extra{k}")
+                    if r == 1:
+                        add_and_store(0, t0, width, held[0], held[1])
 
         for c, width in enumerate(CHUNKS_SECOND):
             t0 = sum(CHUNKS_SECOND[:c])

@@ -22,48 +22,51 @@ P = 128
 PACK = 4
 PASSES = K // (P * PACK)
 HALVES = N // P
+CHOICES = 2
 PER_COL = 16
+QUADRANT = 32
+SCALE_ROWS = 4
+LINE = 4
+BANK_BLOCKS = 4
 GATE_COLS = T // P
+
 GROUP = 2
 LEAD = 2
+WIDE = 5
 SPLIT = 3
-EARLY = 5
-RELU_LAG_WIDE = 2
+POS_AFTER = 3
+SUM_BANKS = 6
+CODE_BUFS = 4
 RELU_LAG_FIRST = 3
 RELU_LAG_SECOND = 2
 CHUNKS_FIRST = (512, 512, 512)
-CHUNKS_SECOND = (512, 512, 256, 256)
-
-
-def unit_order():
-    first = [(e, 0, HALVES if e < EARLY else 1) for e in range(E)]
-    return first + [(e, 1, 1) for e in range(EARLY, E)]
+CHUNKS_SECOND = (512, 512, 384, 128)
 
 
 def tile_moe_pkd_lin_relu_kernel(tc, x_words, x_scales, w, b, gate, offs, pos1, pos2, out):
     nc = tc.nc
-    units = unit_order()
-    last_first = E - 1
+    units = [(e, 0, HALVES if e < WIDE else 1) for e in range(E)] + [(e, 1, 1) for e in range(WIDE, E)]
+    last_first, last_unit = E - 1, len(units) - 1
 
     with ExitStack() as ctx:
         lists = ctx.enter_context(tc.tile_pool(name="lists", bufs=1))
         keep = ctx.enter_context(tc.tile_pool(name="keep", bufs=1))
-        ring = ctx.enter_context(tc.tile_pool(name="ring", bufs=4))
-        gate_psum = ctx.enter_context(tc.psum_pool(name="gate_psum", bufs=2))
-        sum_psum = ctx.enter_context(tc.psum_pool(name="sum_psum", bufs=6))
+        ring = ctx.enter_context(tc.tile_pool(name="ring", bufs=CODE_BUFS))
+        turn_psum = ctx.enter_context(tc.psum_pool(name="turn_psum", bufs=2))
+        sum_psum = ctx.enter_context(tc.psum_pool(name="sum_psum", bufs=1))
 
         offs_sb = lists.tile([P, SLOTS // PER_COL], U16, name="offs_sb")
         nc.sync.dma_start(offs_sb[:], offs)
 
         xs_sb = keep.tile([P, T], U8, name="xs_sb", align_bytes=64)
         nc.vector.memset(xs_sb[:].bitcast(I32), 0)
-        for quad in range(4):
+        for q in range(P // QUADRANT):
             nc.sync.dma_start(
-                out=xs_sb[32 * quad : 32 * quad + 4 * PASSES, :].bitcast(I32),
-                in_=x_scales[:, 4 * quad : 4 * quad + 4, :].bitcast(I32),
+                out=xs_sb[QUADRANT * q : QUADRANT * q + SCALE_ROWS * PASSES, :].bitcast(I32),
+                in_=x_scales[:, SCALE_ROWS * q : SCALE_ROWS * (q + 1), :].bitcast(I32),
             )
 
-        gate_col = keep.tile([P, 2, GATE_COLS], F32, name="gate_col")
+        gate_col = keep.tile([P, CHOICES, GATE_COLS], F32, name="gate_col")
         nc.sync.dma_start(out=gate_col[:], in_=gate[:, 0, :].rearrange("r (p c) -> p r c", p=P))
 
         xw_sb = [keep.tile([P, T], I32, name=f"xw{o}", align_bytes=64) for o in range(PASSES)]
@@ -74,7 +77,7 @@ def tile_moe_pkd_lin_relu_kernel(tc, x_words, x_scales, w, b, gate, offs, pos1, 
         load_words(0)
         raw = {}
         bias = keep.tile([P, HALVES, E], F32, name="bias")
-        pos_sb = [lists.tile([P, T // PER_COL], U16, name=f"pos{r}_sb") for r in range(2)]
+        pos_sb = [lists.tile([P, T // PER_COL], U16, name=f"pos{r}_sb") for r in range(CHOICES)]
         rows = w.rearrange("e (o p j) n -> e o p j n", o=PASSES, j=PACK)
         for e in range(E - SPLIT):
             both = keep.tile([P, PASSES, PACK, N], F32, name=f"raw{e}")
@@ -85,7 +88,7 @@ def tile_moe_pkd_lin_relu_kernel(tc, x_words, x_scales, w, b, gate, offs, pos1, 
             if e == 0:
                 load_words(1)
                 nc.sync.dma_start(out=bias[:], in_=b.rearrange("(h p) e -> p h e", p=P))
-            if e == 3:
+            if e == POS_AFTER:
                 nc.sync.dma_start(pos_sb[0][:], pos1)
                 nc.sync.dma_start(pos_sb[1][:], pos2)
         for h in range(HALVES):
@@ -97,49 +100,66 @@ def tile_moe_pkd_lin_relu_kernel(tc, x_words, x_scales, w, b, gate, offs, pos1, 
 
         ident = keep.tile([P, P], F32, name="ident")
         make_identity(nc, ident[:])
-        gate_sb = [keep.tile([P, T], F32, name=f"gate{r}") for r in range(2)]
-        for r in range(2):
-            for c0 in range(0, GATE_COLS, 4):
-                spread = gate_psum.tile([P, 4, P], F32, name="spread")
-                for j in range(4):
+        gate_sb = [keep.tile([P, T], F32, name=f"gate{r}") for r in range(CHOICES)]
+        for r in range(CHOICES):
+            for c0 in range(0, GATE_COLS, BANK_BLOCKS):
+                spread = turn_psum.tile([P, BANK_BLOCKS, P], F32, name="spread", tag="turn")
+                for j in range(BANK_BLOCKS):
                     nc.tensor.transpose(spread[:, j, :], gate_col[:, r, c0 + j : c0 + j + 1].to_broadcast([P, P]), ident[:])
                 nc.scalar.copy(
-                    out=gate_sb[r][:].rearrange("m (k c) -> m k c", c=GATE_COLS)[:, :, c0 : c0 + 4],
-                    in_=spread[:].rearrange("m j k -> m k j"),
+                    out=gate_sb[r][:].rearrange("m (p c) -> m p c", c=GATE_COLS)[:, :, c0 : c0 + BANK_BLOCKS],
+                    in_=spread[:].rearrange("m j p -> m p j"),
                 )
+
+        def bf16_of(i):
+            return f"bf16_{i}"
+
+        def scales_of(i):
+            return f"scales_{i}"
+
+        def bank_of(i):
+            return f"bank{i % SUM_BANKS}"
 
         y_sb = [keep.tile([P, SLOTS], F32, name=f"y{h}") for h in range(HALVES)]
         tok_words, tok_scales, sums = {}, {}, {}
 
-        def gather_tokens(g, words_tag, scales_tag):
-            width = GROUP * C
-            slots = offs_sb[:, g * width // PER_COL : (g + 1) * width // PER_COL]
-            scales = keep.tile([P, width], U8, name=f"tok_scales{g}", tag=scales_tag, align_bytes=64)
-            nc.vector.tensor_copy(scales[:], xs_sb[:].indirect(slots))
-            words = keep.tile([P, PASSES * width], U32, name=f"tok_words{g}", tag=words_tag, align_bytes=64)
-            for o in range(PASSES):
-                nc.vector.tensor_copy(words[:, o * width : (o + 1) * width], xw_sb[o][:].bitcast(U32).indirect(slots))
+        def slots_of(g):
+            return offs_sb[:, g * GROUP * C // PER_COL : (g + 1) * GROUP * C // PER_COL]
+
+        def gather_scales(g, tag):
+            scales = keep.tile([P, GROUP * C], U8, name=f"tok_scales{g}", tag=tag, align_bytes=64)
+            nc.vector.tensor_copy(scales[:], xs_sb[:].indirect(slots_of(g)))
             for k in range(GROUP):
                 tok_scales[g * GROUP + k] = scales[:, k * C : (k + 1) * C]
+
+        def gather_words(g, tag):
+            width = GROUP * C
+            words = keep.tile([P, PASSES * width], U32, name=f"tok_words{g}", tag=tag, align_bytes=64)
+            for o in range(PASSES):
+                nc.vector.tensor_copy(words[:, o * width : (o + 1) * width], xw_sb[o][:].bitcast(U32).indirect(slots_of(g)))
+            for k in range(GROUP):
                 tok_words[g * GROUP + k] = [words[:, o * width + k * C : o * width + (k + 1) * C] for o in range(PASSES)]
 
         def multiply(i):
             e, h0, count = units[i]
             cols = count * P
-            grouped = keep.tile([P, PASSES, cols, PACK], BF16, name=f"grouped{i}", tag=f"wide{i}", align_bytes=64)
-            dst = grouped[:].rearrange("p o (c i) j -> p o c j i", i=4)
-            src = raw[e, h0][:, :, :, :cols].rearrange("p o j (c i) -> p o c j i", i=4)
-            if i == last_first:
+            on_vector = i == last_first
+            grouped = keep.tile(
+                [P, PASSES, cols, PACK], BF16, name=f"grouped{i}", tag=bf16_of(i - 2 if on_vector else i), align_bytes=64
+            )
+            dst = grouped[:].rearrange("p o (c i) j -> p o c j i", i=LINE)
+            src = raw[e, h0][:, :, :, :cols].rearrange("p o j (c i) -> p o c j i", i=LINE)
+            if on_vector:
                 for o in range(PASSES):
                     nc.vector.tensor_copy(out=dst[:, o], in_=src[:, o])
             else:
                 nc.scalar.copy(out=dst, in_=src)
             codes = ring.tile([P, PASSES * cols], U32, name="codes", align_bytes=64)
-            w_scales = keep.tile([P, PASSES * cols], U8, name=f"w_scales{i}", tag=f"narrow{i}", align_bytes=64)
+            w_scales = keep.tile([P, PASSES * cols], U8, name=f"w_scales{i}", tag=scales_of(i), align_bytes=64)
             nc.vector.quantize_mx(
                 out=codes[:].bitcast(FP8X4), scales=w_scales[:], in_=grouped[:].rearrange("p o n j -> p (o n j)")
             )
-            acc = sum_psum.tile([P, count, C], F32, name="acc")
+            acc = sum_psum.tile([P, count, C], F32, name=f"acc{i}", tag=bank_of(i))
             for k in range(count):
                 for o in range(PASSES):
                     w_cols = slice(o * cols + k * P, o * cols + (k + 1) * P)
@@ -148,7 +168,7 @@ def tile_moe_pkd_lin_relu_kernel(tc, x_words, x_scales, w, b, gate, offs, pos1, 
                         lhsT=codes[:, w_cols].bitcast(FP8X4),
                         lhsT_scale=w_scales[:, w_cols],
                         rhs=tok_words[e][o].bitcast(FP8X4),
-                        rhs_scale=tok_scales[e][4 * o : P, :],
+                        rhs_scale=tok_scales[e][SCALE_ROWS * o : P, :],
                         start=(o == 0),
                         stop=(o == PASSES - 1),
                     )
@@ -172,33 +192,60 @@ def tile_moe_pkd_lin_relu_kernel(tc, x_words, x_scales, w, b, gate, offs, pos1, 
             nc.vector.tensor_tensor(part[:], y_sb[h][:].indirect(picks), gate_sb[r][:, t0 : t0 + width], ALU.mult)
             return part
 
-        def add_and_store(h, t0, width, first, second):
+        def add_on_vector_and_store(h, t0, width, first, second):
             nc.vector.tensor_tensor(first[:], first[:], second[:], ALU.add)
             nc.sync.dma_start(out=out[h * P : (h + 1) * P, t0 : t0 + width], in_=first[:])
 
-        for g in range(LEAD):
-            gather_tokens(g, f"first_words{g}", f"first_scales{g}")
+        def add_on_tensor_and_store(h, t0, width, first, second, bank):
+            blocks = width // P
+            turned = sum_psum.tile([P, blocks, P], F32, name=f"turned{h}_{t0}", tag=bank)
+            for j in range(blocks):
+                for r, part in enumerate((first, second)):
+                    nc.tensor.matmul(
+                        turned[:, j, :], part[:, j * P : (j + 1) * P], ident[:], start=(r == 0), stop=(r == 1), is_transpose=True
+                    )
+            nc.scalar.copy(out=second[:], in_=turned[:].rearrange("p j n -> p (j n)"))
+            back = turn_psum.tile([P, blocks, P], F32, name="back", tag="turn")
+            for j in range(blocks):
+                nc.tensor.transpose(back[:, j, :], second[:, j * P : (j + 1) * P], ident[:])
+            nc.scalar.copy(out=first[:], in_=back[:].rearrange("p j t -> p (j t)"))
+            nc.scalar.dma_start(out=out[h * P : (h + 1) * P, t0 : t0 + width], in_=first[:])
 
-        jobs = [(sum(CHUNKS_FIRST[:c]), width, r) for c, width in enumerate(CHUNKS_FIRST) for r in range(2)]
-        job_at = [min(last_first + 1 + k, len(units) - 1) for k in range(len(jobs))]
+        for g in range(LEAD):
+            gather_scales(g, f"first_scales{g}")
+        for g in range(LEAD):
+            gather_words(g, f"first_words{g}")
+
+        fetches = [(sum(CHUNKS_FIRST[:c]), width, r) for c, width in enumerate(CHUNKS_FIRST) for r in range(CHOICES)]
+        fetch_at = [E + round(k * (last_unit - E) / (len(fetches) - 1)) for k in range(len(fetches))]
+        add_in_bank_of = {c: fetch_at[CHOICES * c + 1] + 2 for c in range(len(CHUNKS_FIRST) - 1)}
         relu_at = [
-            min(i + (RELU_LAG_WIDE if i < EARLY else RELU_LAG_FIRST), last_first + 1) if i <= last_first else min(i + RELU_LAG_SECOND, len(units) - 1)
+            min(i + RELU_LAG_FIRST, last_first) if i <= last_first else min(i + RELU_LAG_SECOND, last_unit)
             for i in range(len(units))
         ]
-        held = {}
+        fetched = {}
         for i in range(len(units)):
             multiply(i)
             if i % GROUP == 0 and LEAD + i // GROUP < E // GROUP:
-                gather_tokens(LEAD + i // GROUP, f"wide{i}", f"narrow{i}")
+                gather_words(LEAD + i // GROUP, bf16_of(i))
+                gather_scales(LEAD + i // GROUP, scales_of(i))
             for done in range(len(units)):
                 if relu_at[done] == i:
                     finish(done)
-            for k, (t0, width, r) in enumerate(jobs):
-                if job_at[k] == i:
-                    held[r] = weighted(0, r, t0, width, f"wide{i}" if last_first + 1 + k == i else f"extra{k}")
-                    if r == 1:
-                        add_and_store(0, t0, width, held[0], held[1])
+            for k, (t0, width, r) in enumerate(fetches):
+                if fetch_at[k] == i:
+                    fetched[k] = weighted(0, r, t0, width, bf16_of(i))
+                    if k == len(fetches) - 1:
+                        add_on_vector_and_store(0, t0, width, fetched[k - 1], fetched[k])
+            for c, unit in add_in_bank_of.items():
+                if relu_at[unit] == i:
+                    k = CHOICES * c
+                    add_on_tensor_and_store(0, fetches[k][0], fetches[k][1], fetched[k], fetched[k + 1], bank_of(unit))
 
         for c, width in enumerate(CHUNKS_SECOND):
             t0 = sum(CHUNKS_SECOND[:c])
-            add_and_store(1, t0, width, *[weighted(1, r, t0, width, f"last{c}_{r}") for r in range(2)])
+            parts = [weighted(1, r, t0, width, f"last{c}_{r}") for r in range(CHOICES)]
+            if c == 0:
+                add_on_tensor_and_store(1, t0, width, *parts, bank_of(last_unit - 1))
+            else:
+                add_on_vector_and_store(1, t0, width, *parts)

from contextlib import ExitStack

import concourse.mybir as mybir
from concourse.masks import make_identity

K, T, E, C, N = 1024, 1536, 12, 256, 256
SLOTS = E * C
FLOPS = 2 * K * N * SLOTS
BYTES = K * T + K * T // 32 + 4 * E * K * N + 4 * N * E + 4 * 2 * T + 2 * 128 * (SLOTS + 2 * T) // 16 + 4 * N * T

F32 = mybir.dt.float32
BF16 = mybir.dt.bfloat16
I32 = mybir.dt.int32
U32 = mybir.dt.uint32
U16 = mybir.dt.uint16
U8 = mybir.dt.uint8
FP8X4 = mybir.dt.float8_e4m3fn_x4
ACT = mybir.ActivationFunctionType
ALU = mybir.AluOpType

P = 128
PACK = 4
PASSES = K // (P * PACK)
HALVES = N // P
CHOICES = 2
PER_COL = 16
QUADRANT = 32
SCALE_ROWS = 4
LINE = 4
BANK_BLOCKS = 4
GATE_COLS = T // P

GROUP = 2
LEAD = 2
WIDE = 5
SPLIT = 3
POS_AFTER = 3
SUM_BANKS = 6
CODE_BUFS = 4
RELU_LAG_FIRST = 3
RELU_LAG_SECOND = 2
CHUNKS_FIRST = (512, 512, 512)
CHUNKS_SECOND = (512, 512, 384, 128)


def tile_moe_pkd_lin_relu_kernel(tc, x_words, x_scales, w, b, gate, offs, pos1, pos2, out):
    nc = tc.nc
    units = [(e, 0, HALVES if e < WIDE else 1) for e in range(E)] + [(e, 1, 1) for e in range(WIDE, E)]
    last_first, last_unit = E - 1, len(units) - 1

    with ExitStack() as ctx:
        lists = ctx.enter_context(tc.tile_pool(name="lists", bufs=1))
        keep = ctx.enter_context(tc.tile_pool(name="keep", bufs=1))
        ring = ctx.enter_context(tc.tile_pool(name="ring", bufs=CODE_BUFS))
        turn_psum = ctx.enter_context(tc.psum_pool(name="turn_psum", bufs=2))
        sum_psum = ctx.enter_context(tc.psum_pool(name="sum_psum", bufs=1))

        offs_sb = lists.tile([P, SLOTS // PER_COL], U16, name="offs_sb")
        nc.sync.dma_start(offs_sb[:], offs)

        xs_sb = keep.tile([P, T], U8, name="xs_sb", align_bytes=64)
        nc.vector.memset(xs_sb[:].bitcast(I32), 0)
        for q in range(P // QUADRANT):
            nc.sync.dma_start(
                out=xs_sb[QUADRANT * q : QUADRANT * q + SCALE_ROWS * PASSES, :].bitcast(I32),
                in_=x_scales[:, SCALE_ROWS * q : SCALE_ROWS * (q + 1), :].bitcast(I32),
            )

        gate_col = keep.tile([P, CHOICES, GATE_COLS], F32, name="gate_col")
        nc.sync.dma_start(out=gate_col[:], in_=gate[:, 0, :].rearrange("r (p c) -> p r c", p=P))

        xw_sb = [keep.tile([P, T], I32, name=f"xw{o}", align_bytes=64) for o in range(PASSES)]

        def load_words(o):
            nc.sync.dma_start(out=xw_sb[o][:], in_=x_words[o].rearrange("p t r -> p (t r)").bitcast(I32))

        load_words(0)
        raw = {}
        bias = keep.tile([P, HALVES, E], F32, name="bias")
        pos_sb = [lists.tile([P, T // PER_COL], U16, name=f"pos{r}_sb") for r in range(CHOICES)]
        rows = w.rearrange("e (o p j) n -> e o p j n", o=PASSES, j=PACK)
        for e in range(E - SPLIT):
            both = keep.tile([P, PASSES, PACK, N], F32, name=f"raw{e}")
            for o in range(PASSES):
                nc.sync.dma_start(out=both[:, o], in_=rows[e, o])
            for h in range(HALVES):
                raw[e, h] = both[:, :, :, h * P :]
            if e == 0:
                load_words(1)
                nc.sync.dma_start(out=bias[:], in_=b.rearrange("(h p) e -> p h e", p=P))
            if e == POS_AFTER:
                nc.sync.dma_start(pos_sb[0][:], pos1)
                nc.sync.dma_start(pos_sb[1][:], pos2)
        for h in range(HALVES):
            for e in range(E - SPLIT, E):
                half = keep.tile([P, PASSES, PACK, P], F32, name=f"raw{e}_{h}")
                for o in range(PASSES):
                    nc.sync.dma_start(out=half[:, o], in_=rows[e, o, :, :, h * P : (h + 1) * P])
                raw[e, h] = half[:]

        ident = keep.tile([P, P], F32, name="ident")
        make_identity(nc, ident[:])
        gate_sb = [keep.tile([P, T], F32, name=f"gate{r}") for r in range(CHOICES)]
        for r in range(CHOICES):
            for c0 in range(0, GATE_COLS, BANK_BLOCKS):
                spread = turn_psum.tile([P, BANK_BLOCKS, P], F32, name="spread", tag="turn")
                for j in range(BANK_BLOCKS):
                    nc.tensor.transpose(spread[:, j, :], gate_col[:, r, c0 + j : c0 + j + 1].to_broadcast([P, P]), ident[:])
                nc.scalar.copy(
                    out=gate_sb[r][:].rearrange("m (p c) -> m p c", c=GATE_COLS)[:, :, c0 : c0 + BANK_BLOCKS],
                    in_=spread[:].rearrange("m j p -> m p j"),
                )

        def bf16_of(i):
            return f"bf16_{i}"

        def scales_of(i):
            return f"scales_{i}"

        def bank_of(i):
            return f"bank{i % SUM_BANKS}"

        y_sb = [keep.tile([P, SLOTS], F32, name=f"y{h}") for h in range(HALVES)]
        tok_words, tok_scales, sums = {}, {}, {}

        def slots_of(g):
            return offs_sb[:, g * GROUP * C // PER_COL : (g + 1) * GROUP * C // PER_COL]

        def gather_scales(g, tag):
            scales = keep.tile([P, GROUP * C], U8, name=f"tok_scales{g}", tag=tag, align_bytes=64)
            nc.vector.tensor_copy(scales[:], xs_sb[:].indirect(slots_of(g)))
            for k in range(GROUP):
                tok_scales[g * GROUP + k] = scales[:, k * C : (k + 1) * C]

        def gather_words(g, tag):
            width = GROUP * C
            words = keep.tile([P, PASSES * width], U32, name=f"tok_words{g}", tag=tag, align_bytes=64)
            for o in range(PASSES):
                nc.vector.tensor_copy(words[:, o * width : (o + 1) * width], xw_sb[o][:].bitcast(U32).indirect(slots_of(g)))
            for k in range(GROUP):
                tok_words[g * GROUP + k] = [words[:, o * width + k * C : o * width + (k + 1) * C] for o in range(PASSES)]

        def multiply(i):
            e, h0, count = units[i]
            cols = count * P
            on_vector = i == last_first
            grouped = keep.tile(
                [P, PASSES, cols, PACK], BF16, name=f"grouped{i}", tag=bf16_of(i - 2 if on_vector else i), align_bytes=64
            )
            dst = grouped[:].rearrange("p o (c i) j -> p o c j i", i=LINE)
            src = raw[e, h0][:, :, :, :cols].rearrange("p o j (c i) -> p o c j i", i=LINE)
            if on_vector:
                for o in range(PASSES):
                    nc.vector.tensor_copy(out=dst[:, o], in_=src[:, o])
            else:
                nc.scalar.copy(out=dst, in_=src)
            codes = ring.tile([P, PASSES * cols], U32, name="codes", align_bytes=64)
            w_scales = keep.tile([P, PASSES * cols], U8, name=f"w_scales{i}", tag=scales_of(i), align_bytes=64)
            nc.vector.quantize_mx(
                out=codes[:].bitcast(FP8X4), scales=w_scales[:], in_=grouped[:].rearrange("p o n j -> p (o n j)")
            )
            acc = sum_psum.tile([P, count, C], F32, name=f"acc{i}", tag=bank_of(i))
            for k in range(count):
                for o in range(PASSES):
                    w_cols = slice(o * cols + k * P, o * cols + (k + 1) * P)
                    nc.tensor.matmul_mx(
                        out=acc[:, k, :],
                        lhsT=codes[:, w_cols].bitcast(FP8X4),
                        lhsT_scale=w_scales[:, w_cols],
                        rhs=tok_words[e][o].bitcast(FP8X4),
                        rhs_scale=tok_scales[e][SCALE_ROWS * o : P, :],
                        start=(o == 0),
                        stop=(o == PASSES - 1),
                    )
            sums[i] = acc

        def finish(i):
            e, h0, count = units[i]
            for k in range(count):
                h = h0 + k
                nc.scalar.activation(
                    out=y_sb[h][:, e * C : (e + 1) * C],
                    in_=sums[i][:, k, :],
                    func=ACT.Relu,
                    bias=bias[:, h, e : e + 1],
                    scale=1.0,
                )

        def weighted(h, r, t0, width, tag):
            part = keep.tile([P, width], F32, name=f"part{h}_{r}_{t0}", tag=tag, align_bytes=64)
            picks = pos_sb[r][:, t0 // PER_COL : (t0 + width) // PER_COL]
            nc.vector.tensor_tensor(part[:], y_sb[h][:].indirect(picks), gate_sb[r][:, t0 : t0 + width], ALU.mult)
            return part

        def add_on_vector_and_store(h, t0, width, first, second):
            nc.vector.tensor_tensor(first[:], first[:], second[:], ALU.add)
            nc.sync.dma_start(out=out[h * P : (h + 1) * P, t0 : t0 + width], in_=first[:])

        def add_on_tensor_and_store(h, t0, width, first, second, bank):
            blocks = width // P
            turned = sum_psum.tile([P, blocks, P], F32, name=f"turned{h}_{t0}", tag=bank)
            for j in range(blocks):
                for r, part in enumerate((first, second)):
                    nc.tensor.matmul(
                        turned[:, j, :], part[:, j * P : (j + 1) * P], ident[:], start=(r == 0), stop=(r == 1), is_transpose=True
                    )
            nc.scalar.copy(out=second[:], in_=turned[:].rearrange("p j n -> p (j n)"))
            back = turn_psum.tile([P, blocks, P], F32, name="back", tag="turn")
            for j in range(blocks):
                nc.tensor.transpose(back[:, j, :], second[:, j * P : (j + 1) * P], ident[:])
            nc.scalar.copy(out=first[:], in_=back[:].rearrange("p j t -> p (j t)"))
            nc.scalar.dma_start(out=out[h * P : (h + 1) * P, t0 : t0 + width], in_=first[:])

        for g in range(LEAD):
            gather_scales(g, f"first_scales{g}")
        for g in range(LEAD):
            gather_words(g, f"first_words{g}")

        fetches = [(sum(CHUNKS_FIRST[:c]), width, r) for c, width in enumerate(CHUNKS_FIRST) for r in range(CHOICES)]
        fetch_at = [E + round(k * (last_unit - E) / (len(fetches) - 1)) for k in range(len(fetches))]
        add_in_bank_of = {c: fetch_at[CHOICES * c + 1] + 2 for c in range(len(CHUNKS_FIRST) - 1)}
        relu_at = [
            min(i + RELU_LAG_FIRST, last_first) if i <= last_first else min(i + RELU_LAG_SECOND, last_unit)
            for i in range(len(units))
        ]
        fetched = {}
        for i in range(len(units)):
            multiply(i)
            if i % GROUP == 0 and LEAD + i // GROUP < E // GROUP:
                gather_words(LEAD + i // GROUP, bf16_of(i))
                gather_scales(LEAD + i // GROUP, scales_of(i))
            for done in range(len(units)):
                if relu_at[done] == i:
                    finish(done)
            for k, (t0, width, r) in enumerate(fetches):
                if fetch_at[k] == i:
                    fetched[k] = weighted(0, r, t0, width, bf16_of(i))
                    if k == len(fetches) - 1:
                        add_on_vector_and_store(0, t0, width, fetched[k - 1], fetched[k])
            for c, unit in add_in_bank_of.items():
                if relu_at[unit] == i:
                    k = CHOICES * c
                    add_on_tensor_and_store(0, fetches[k][0], fetches[k][1], fetched[k], fetched[k + 1], bank_of(unit))

        for c, width in enumerate(CHUNKS_SECOND):
            t0 = sum(CHUNKS_SECOND[:c])
            parts = [weighted(1, r, t0, width, f"last{c}_{r}") for r in range(CHOICES)]
            if c == 0:
                add_on_tensor_and_store(1, t0, width, *parts, bank_of(last_unit - 1))
            else:
                add_on_vector_and_store(1, t0, width, *parts)
